import numpy as np
import ml_dtypes


def mxq(x, axis, fmt="e4m3"):
    dtype, down = {"e4m3": (ml_dtypes.float8_e4m3fn, 7), "e5m2": (ml_dtypes.float8_e5m2, 14)}[fmt]
    v = np.moveaxis(np.asarray(x, np.float32).astype(ml_dtypes.bfloat16).astype(np.float64), axis, -1)
    blocks = v.reshape(v.shape[:-1] + (-1, 32))
    amax = np.abs(blocks).max(-1, keepdims=True)
    byte = np.maximum(np.where(amax > 0, np.frexp(amax)[1] - 1 + 127, 0) - down, 1)
    scale = np.exp2(byte - 127.0)
    codes = (blocks / scale).astype(np.float32).astype(dtype).astype(np.float64)
    return np.moveaxis((codes * scale).reshape(v.shape), -1, axis)


WIDE = False


def mx_kscale(k):
    if not WIDE:
        return np.ones(k)
    levels = np.array([10, -10, 5, -5, 0])
    if k % 512:
        return np.exp2(np.random.permutation(np.resize(levels, k // 32))).repeat(32)
    a = np.empty((k // 512, 16))
    for p in range(k // 512):
        a[p, :8] = np.random.permutation(np.resize(levels, 8))
        for g in range(8):
            far = levels[np.abs(levels - a[p, g]) >= 10]
            a[p, g + 8] = far[np.random.randint(len(far))]
    return np.exp2(a.ravel()).repeat(32)


def f64(x):
    return np.asarray(x).astype(np.float64)


def striped(idx):
    return np.tile(idx.reshape(-1, 16).T, (8, 1)).astype(np.uint16)


def unstriped(offs):
    return offs[:16].T.reshape(-1).astype(np.int64)


def pack_weight(w):
    k, n = w.shape
    w = f64(np.asarray(w, np.float32).astype(ml_dtypes.bfloat16)).reshape(k // 32, 32, n)
    amax = np.abs(w).max(1)
    byte = np.clip(np.where(amax > 0, np.frexp(amax)[1] - 1 + 127 - 7, 1), 1, 254)
    scaled = (w * np.exp2(127.0 - byte)[:, None, :]).reshape(k, n).astype(np.float32)
    words = np.ascontiguousarray(scaled.reshape(k // 512, 128, 4, n).transpose(0, 1, 3, 2)).astype(ml_dtypes.float8_e4m3fn).view(np.uint8)
    return words, np.ascontiguousarray(byte.astype(np.uint8).reshape(k // 512, 16, n))


def unpack_weight(words, scales):
    g, p, n, _ = words.shape
    vals = np.ascontiguousarray(words).view(ml_dtypes.float8_e4m3fn).astype(np.float64) * np.repeat(np.exp2(scales.astype(np.float64) - 127.0), 8, axis=1)[..., None]
    return vals.transpose(0, 1, 3, 2).reshape(g * 512, n)


def sigmoid(v):
    return 1.0 / (1.0 + np.exp(-np.maximum(v, -700.0)))


K, T, S, V = 512, 1024, 512, 512


def setup_inputs():
    n = np.random.standard_normal
    s = mx_kscale(K)[:, None]
    packed_xT = pack_weight(n((K, T)) * s)
    return {
        "x_words": packed_xT[0],
        "x_scales": packed_xT[1],
        "hT": (n((K, V)) / np.sqrt(K) / s).astype(np.float32),
        "offs": striped(np.random.permutation(T)[:S]),
    }


def reference(x_words, x_scales, hT, offs):
    hTq = mxq(f64(hT), 0, "e4m3")
    xq = unpack_weight(x_words, x_scales)[:, unstriped(offs)]
    y = 1.5 * (hTq.T @ xq)
    ex = np.exp(y)
    ls = np.log(ex.sum(axis=1, keepdims=True))
    lp = y - ls
    pr = np.exp(lp)
    pl = pr * lp
    negh = pl.sum(axis=1, keepdims=True)
    dev = np.abs(lp - negh)
    md = dev.mean(axis=1, keepdims=True)
    return (100.0 * pr) * (sigmoid(-4.0 * (dev - (0.8 * md))))

@@ -1,0 +1,158 @@
+from contextlib import ExitStack
+
+import concourse.mybir as mybir
+
+K, T, S, V = 512, 1024, 512, 512
+FLOPS = 2 * K * S * V
+
+F32 = mybir.dt.float32
+BF16 = mybir.dt.bfloat16
+I32 = mybir.dt.int32
+U32 = mybir.dt.uint32
+U16 = mybir.dt.uint16
+U8 = mybir.dt.uint8
+FP8X4 = mybir.dt.float8_e4m3fn_x4
+ALU = mybir.AluOpType
+ACT = mybir.ActivationFunctionType
+
+P = 128
+PACK = 4
+TILES = V // P
+HALF = S // 2
+BIAS_PER_SUM = 0.5 * 4.0 * 0.8 / S
+
+
+def tile_picked_ytyp_loc_p_kernel(tc, x_words, x_scales, hT, offs, out):
+    nc = tc.nc
+    with ExitStack() as ctx:
+        keep = ctx.enter_context(tc.tile_pool(name="keep", bufs=1))
+        psum = ctx.enter_context(tc.psum_pool(name="psum", bufs=1))
+
+        offsets = keep.tile([P, S // 16], U16, name="offsets")
+        words = keep.tile([P, T], I32, name="words", align_bytes=64)
+        plane = keep.tile([P, T], U8, name="plane", align_bytes=64)
+        warm = keep.tile([P, 2], F32, name="warm")
+
+        nc.vector.memset(plane[:].bitcast(I32), 0)
+        nc.vector.memset(warm[:, 0:1], 0.0)
+        nc.sync.dma_start(offsets[:], offs)
+        for q in range(4):
+            nc.scalar.dma_start(plane[32 * q : 32 * q + 4, :].bitcast(I32), x_scales[0, 4 * q : 4 * q + 4, :].bitcast(I32))
+        nc.scalar.activation(warm[:, 1:2], warm[:, 0:1], ACT.Exp)
+        h_rows = hT.rearrange("(p j) w -> p j w", j=PACK)
+        raw0 = keep.tile([P, PACK, P], F32, name="raw0")
+        raw1 = keep.tile([P, PACK, P], F32, name="raw1")
+        raw2 = keep.tile([P, PACK, 2 * P], F32, name="raw2")
+        nc.sync.dma_start(words[:], x_words[0].rearrange("p n t -> p (n t)").bitcast(I32))
+        nc.sync.dma_start(raw0[:], h_rows[:, :, 0:P])
+        nc.sync.dma_start(raw1[:], h_rows[:, :, P : 2 * P])
+        nc.sync.dma_start(raw2[:], h_rows[:, :, 2 * P : V])
+        h_raw = [raw0[:], raw1[:], raw2[:, :, 0:P], raw2[:, :, P : 2 * P]]
+
+        x_bytes = keep.tile([P, S], U8, name="x_bytes", align_bytes=64)
+        x_codes = keep.tile([P, S], U32, name="x_codes", align_bytes=64)
+        nc.vector.tensor_copy(x_codes[:], words[:].bitcast(U32).indirect(offsets[:]))
+
+        h_codes, h_bytes = [], []
+
+        def quantise(i):
+            src = h_raw[i]
+            grouped = keep.tile([P, P * PACK], BF16, name="grouped%d" % i, align_bytes=64)
+            nc.scalar.copy(
+                grouped[:].rearrange("p (c i t) -> p c t i", i=4, t=PACK),
+                src.rearrange("p t (c i) -> p c t i", i=4),
+            )
+            codes = keep.tile([P, P], U32, name="h_codes%d" % i, align_bytes=64)
+            scales = keep.tile([P, P], U8, name="h_bytes%d" % i, align_bytes=64)
+            nc.vector.quantize_mx(out=codes[:].bitcast(FP8X4), scales=scales[:], in_=grouped[:])
+            h_codes.append(codes)
+            h_bytes.append(scales)
+
+        def product(i, acc, cols):
+            nc.tensor.matmul_mx(
+                out=acc,
+                lhsT=h_codes[i][:].bitcast(FP8X4),
+                lhsT_scale=h_bytes[i][:],
+                rhs=x_codes[:, cols].bitcast(FP8X4),
+                rhs_scale=x_bytes[:, cols],
+                start=True,
+                stop=True,
+            )
+
+        neg_y = [keep.tile([P, S], F32, name="neg_y%d" % i) for i in range(TILES)]
+        ex = [keep.tile([P, S], F32, name="ex%d" % i) for i in range(TILES)]
+        pr = [keep.tile([P, S], F32, name="pr%d" % i) for i in range(TILES)]
+        junk = [keep.tile([P, S], F32, name="junk%d" % i) for i in range(TILES)]
+        dev = [keep.tile([P, S], F32, name="dev%d" % i) for i in range(TILES)]
+        soft = [keep.tile([P, S], F32, name="soft%d" % i) for i in range(TILES)]
+        res = [keep.tile([P, S], F32, name="res%d" % i) for i in range(TILES)]
+
+        def column(label, i):
+            return keep.tile([P, 1], F32, name="%s%d" % (label, i))
+
+        neg_max = [column("neg_max", i) for i in range(TILES)]
+        total = [column("total", i) for i in range(TILES)]
+        inv = [column("inv", i) for i in range(TILES)]
+        inv_k = [column("inv_k", i) for i in range(TILES)]
+        centre = [column("centre", i) for i in range(TILES)]
+        level = [column("level", i) for i in range(TILES)]
+
+        acc = [psum.tile([P, S], F32, name="acc%d" % i) for i in range(TILES)]
+        halves = [slice(0, HALF), slice(HALF, S)]
+        quantise(0)
+        for u, cols in enumerate(halves):
+            nc.vector.tensor_copy(
+                x_bytes[:, cols], plane[:].indirect(offsets[:, u * HALF // 16 : (u + 1) * HALF // 16])
+            )
+            product(0, acc[0][:, cols], cols)
+        for i in range(1, TILES):
+            quantise(i)
+            product(i, acc[i][:], slice(0, S))
+
+        def logits(i):
+            nc.vector.tensor_scalar(neg_y[i][:], acc[i][:], -1.5, None, ALU.mult, ALU.min, accum_out=neg_max[i][:])
+
+        def exponent(i):
+            nc.scalar.activation(ex[i][:], neg_y[i][:], ACT.Exp, bias=neg_max[i][:], scale=-1.0, accum_out=total[i][:])
+
+        def centre_of(i):
+            nc.vector.reciprocal(inv[i][:], total[i][:])
+            nc.vector.scalar_tensor_tensor(
+                junk[i][:], acc[i][:], -1.5 * BIAS_PER_SUM, ex[i][:], ALU.mult, ALU.mult, accum_out=inv_k[i][:]
+            )
+            nc.vector.tensor_scalar(centre[i][:], inv_k[i][:], inv[i][:], None, ALU.mult)
+
+        def distance(i):
+            nc.scalar.activation(
+                dev[i][:], neg_y[i][:], ACT.Abs, bias=centre[i][:], scale=-BIAS_PER_SUM, accum_out=level[i][:]
+            )
+
+        def percent(i):
+            nc.gpsimd.tensor_scalar(pr[i][:], ex[i][:], inv[i][:], 50.0, ALU.mult, ALU.mult)
+
+        def choice(i, cols):
+            nc.scalar.activation(soft[i][:, cols], dev[i][:, cols], ACT.Tanh, bias=level[i][:], scale=-2.0 / BIAS_PER_SUM)
+
+        def finish(i, cols):
+            nc.vector.scalar_tensor_tensor(res[i][:, cols], soft[i][:, cols], 1.0, pr[i][:, cols], ALU.add, ALU.mult)
+            nc.sync.dma_start(out[i * P : (i + 1) * P, cols], res[i][:, cols])
+
+        whole = slice(0, S)
+        logits(0)
+        exponent(0)
+        for i in range(TILES):
+            if i + 1 < TILES:
+                logits(i + 1)
+                exponent(i + 1)
+            centre_of(i)
+            percent(i)
+            if i >= 2:
+                choice(i - 2, whole)
+            distance(i)
+        for i in range(TILES - 1):
+            if i >= 2:
+                choice(i, whole)
+            finish(i, whole)
+        for cols in halves:
+            choice(TILES - 1, cols)
+            finish(TILES - 1, cols)

@@ -29,60 +29,59 @@ def tile_picked_ytyp_loc_p_kernel(tc, x_words, x_scales, hT, offs, out):
         psum = ctx.enter_context(tc.psum_pool(name="psum", bufs=1))
 
         offsets = keep.tile([P, S // 16], U16, name="offsets")
-        words = keep.tile([P, T], I32, name="words", align_bytes=64)
-        plane = keep.tile([P, T], U8, name="plane", align_bytes=64)
+        words = keep.tile([P, T], I32, name="words", tag="after_words", align_bytes=64)
+        plane = keep.tile([P, T], U8, name="plane", tag="after_plane", align_bytes=64)
         warm = keep.tile([P, 2], F32, name="warm")
 
         nc.vector.memset(plane[:].bitcast(I32), 0)
         nc.vector.memset(warm[:, 0:1], 0.0)
         nc.sync.dma_start(offsets[:], offs)
-        for q in range(4):
-            nc.scalar.dma_start(plane[32 * q : 32 * q + 4, :].bitcast(I32), x_scales[0, 4 * q : 4 * q + 4, :].bitcast(I32))
         nc.scalar.activation(warm[:, 1:2], warm[:, 0:1], ACT.Exp)
         h_rows = hT.rearrange("(p j) w -> p j w", j=PACK)
         raw0 = keep.tile([P, PACK, P], F32, name="raw0")
-        raw1 = keep.tile([P, PACK, P], F32, name="raw1")
-        raw2 = keep.tile([P, PACK, 2 * P], F32, name="raw2")
-        nc.sync.dma_start(words[:], x_words[0].rearrange("p n t -> p (n t)").bitcast(I32))
+        raw1 = keep.tile([P, PACK, 2 * P], F32, name="raw1")
+        raw2 = keep.tile([P, PACK, P], F32, name="raw2")
         nc.sync.dma_start(raw0[:], h_rows[:, :, 0:P])
-        nc.sync.dma_start(raw1[:], h_rows[:, :, P : 2 * P])
-        nc.sync.dma_start(raw2[:], h_rows[:, :, 2 * P : V])
-        h_raw = [raw0[:], raw1[:], raw2[:, :, 0:P], raw2[:, :, P : 2 * P]]
+        for q in range(4):
+            nc.sync.dma_start(plane[32 * q : 32 * q + 4, :].bitcast(I32), x_scales[0, 4 * q : 4 * q + 4, :].bitcast(I32))
+        nc.sync.dma_start(raw1[:], h_rows[:, :, P : 3 * P])
+        nc.sync.dma_start(words[:], x_words[0].rearrange("p n t -> p (n t)").bitcast(I32))
+        nc.sync.dma_start(raw2[:], h_rows[:, :, 3 * P : V])
 
         x_bytes = keep.tile([P, S], U8, name="x_bytes", align_bytes=64)
         x_codes = keep.tile([P, S], U32, name="x_codes", align_bytes=64)
-        nc.vector.tensor_copy(x_codes[:], words[:].bitcast(U32).indirect(offsets[:]))
+        nc.vector.tensor_copy(x_bytes[:], plane[:].indirect(offsets[:]))
 
         h_codes, h_bytes = [], []
 
-        def quantise(i):
-            src = h_raw[i]
-            grouped = keep.tile([P, P * PACK], BF16, name="grouped%d" % i, align_bytes=64)
+        def quantise(raw, staged_tag, codes_tag):
+            tiles = 1
+            width = P
+            grouped = keep.tile([P, width * PACK], BF16, name="grouped", tag=staged_tag, align_bytes=64)
             nc.scalar.copy(
                 grouped[:].rearrange("p (c i t) -> p c t i", i=4, t=PACK),
-                src.rearrange("p t (c i) -> p c t i", i=4),
+                raw.rearrange("p t (c i) -> p c t i", i=4),
             )
-            codes = keep.tile([P, P], U32, name="h_codes%d" % i, align_bytes=64)
-            scales = keep.tile([P, P], U8, name="h_bytes%d" % i, align_bytes=64)
+            codes = keep.tile([P, width], U32, name="h_codes", tag=codes_tag, align_bytes=64)
+            scales = keep.tile([P, width], U8, name="h_bytes%d" % len(h_codes), align_bytes=64)
             nc.vector.quantize_mx(out=codes[:].bitcast(FP8X4), scales=scales[:], in_=grouped[:])
-            h_codes.append(codes)
-            h_bytes.append(scales)
+            for j in range(tiles):
+                h_codes.append(codes[:, j * P : (j + 1) * P])
+                h_bytes.append(scales[:, j * P : (j + 1) * P])
 
         def product(i, acc, cols):
             nc.tensor.matmul_mx(
                 out=acc,
-                lhsT=h_codes[i][:].bitcast(FP8X4),
-                lhsT_scale=h_bytes[i][:],
+                lhsT=h_codes[i].bitcast(FP8X4),
+                lhsT_scale=h_bytes[i],
                 rhs=x_codes[:, cols].bitcast(FP8X4),
                 rhs_scale=x_bytes[:, cols],
                 start=True,
                 stop=True,
             )
 
-        neg_y = [keep.tile([P, S], F32, name="neg_y%d" % i) for i in range(TILES)]
         ex = [keep.tile([P, S], F32, name="ex%d" % i) for i in range(TILES)]
-        pr = [keep.tile([P, S], F32, name="pr%d" % i) for i in range(TILES)]
-        junk = [keep.tile([P, S], F32, name="junk%d" % i) for i in range(TILES)]
+        junk = [keep.tile([P, S], F32, name="junk%d" % i, tag="junk%d" % i) for i in range(TILES)]
         dev = [keep.tile([P, S], F32, name="dev%d" % i) for i in range(TILES)]
         soft = [keep.tile([P, S], F32, name="soft%d" % i) for i in range(TILES)]
         res = [keep.tile([P, S], F32, name="res%d" % i) for i in range(TILES)]
@@ -98,18 +97,33 @@ def tile_picked_ytyp_loc_p_kernel(tc, x_words, x_scales, hT, offs, out):
         level = [column("level", i) for i in range(TILES)]
 
         acc = [psum.tile([P, S], F32, name="acc%d" % i) for i in range(TILES)]
+        late = psum.tile([P, HALF], F32, name="late")
         halves = [slice(0, HALF), slice(HALF, S)]
-        quantise(0)
+        first = [acc[0][:, halves[0]], late[:]]
+        quantise(raw0[:], "staged0", "after_plane")
+        quantise(raw1[:, :, 0:P], "staged1", "codes1")
         for u, cols in enumerate(halves):
             nc.vector.tensor_copy(
-                x_bytes[:, cols], plane[:].indirect(offsets[:, u * HALF // 16 : (u + 1) * HALF // 16])
+                x_codes[:, cols], words[:].bitcast(U32).indirect(offsets[:, u * HALF // 16 : (u + 1) * HALF // 16])
             )
-            product(0, acc[0][:, cols], cols)
+            product(0, first[u], cols)
+        quantise(raw1[:, :, P : 2 * P], "staged2", "after_words")
+        quantise(raw2[:], "staged3", "codes3")
         for i in range(1, TILES):
-            quantise(i)
             product(i, acc[i][:], slice(0, S))
 
+        neg_y = [
+            keep.tile([P, S], F32, name="neg_y%d" % i, tag="staged3" if i == 0 else "neg_y%d" % i, align_bytes=64)
+            for i in range(TILES)
+        ]
+
+        half_max = column("half_max", 0)
+
         def logits(i):
+            if i == 0:
+                nc.vector.tensor_scalar(neg_y[0][:, halves[0]], first[0], -1.5, None, ALU.mult, ALU.min, accum_out=half_max[:])
+                nc.vector.tensor_scalar(neg_y[0][:, halves[1]], first[1], -1.5, half_max[:], ALU.mult, ALU.min, accum_out=neg_max[0][:])
+                return
             nc.vector.tensor_scalar(neg_y[i][:], acc[i][:], -1.5, None, ALU.mult, ALU.min, accum_out=neg_max[i][:])
 
         def exponent(i):
@@ -117,10 +131,10 @@ def tile_picked_ytyp_loc_p_kernel(tc, x_words, x_scales, hT, offs, out):
 
         def centre_of(i):
             nc.vector.reciprocal(inv[i][:], total[i][:])
+            nc.vector.tensor_scalar(inv_k[i][:], inv[i][:], (1.0 if i == 0 else -1.5) * BIAS_PER_SUM, None, ALU.mult)
             nc.vector.scalar_tensor_tensor(
-                junk[i][:], acc[i][:], -1.5 * BIAS_PER_SUM, ex[i][:], ALU.mult, ALU.mult, accum_out=inv_k[i][:]
+                junk[i][:], neg_y[i][:] if i == 0 else acc[i][:], inv_k[i][:], ex[i][:], ALU.mult, ALU.mult, accum_out=centre[i][:]
             )
-            nc.vector.tensor_scalar(centre[i][:], inv_k[i][:], inv[i][:], None, ALU.mult)
 
         def distance(i):
             nc.scalar.activation(
@@ -128,7 +142,7 @@ def tile_picked_ytyp_loc_p_kernel(tc, x_words, x_scales, hT, offs, out):
             )
 
         def percent(i):
-            nc.gpsimd.tensor_scalar(pr[i][:], ex[i][:], inv[i][:], 50.0, ALU.mult, ALU.mult)
+            nc.vector.tensor_scalar(pr[i], ex[i][:], inv[i][:], 50.0, ALU.mult, ALU.mult)
 
         def choice(i, cols):
             nc.scalar.activation(soft[i][:, cols], dev[i][:, cols], ACT.Tanh, bias=level[i][:], scale=-2.0 / BIAS_PER_SUM)
@@ -138,21 +152,24 @@ def tile_picked_ytyp_loc_p_kernel(tc, x_words, x_scales, hT, offs, out):
             nc.sync.dma_start(out[i * P : (i + 1) * P, cols], res[i][:, cols])
 
         whole = slice(0, S)
-        logits(0)
-        exponent(0)
+        for i in range(2):
+            logits(i)
+            exponent(i)
         for i in range(TILES):
-            if i + 1 < TILES:
-                logits(i + 1)
-                exponent(i + 1)
+            if i + 2 < TILES:
+                logits(i + 2)
+                exponent(i + 2)
             centre_of(i)
-            percent(i)
             if i >= 2:
                 choice(i - 2, whole)
             distance(i)
-        for i in range(TILES - 1):
-            if i >= 2:
-                choice(i, whole)
+        pr_all = keep.tile([P, TILES * S], F32, name="pr_all", tag="junk2")
+        pr = [pr_all[:, i * S : (i + 1) * S] for i in range(TILES)]
+        for i in range(TILES - 2):
+            percent(i)
             finish(i, whole)
-        for cols in halves:
-            choice(TILES - 1, cols)
-            finish(TILES - 1, cols)
+        for i in range(TILES - 2, TILES):
+            percent(i)
+            for cols in halves:
+                choice(i, cols)
+                finish(i, cols)

@@ -82,6 +82,7 @@ def tile_picked_ytyp_loc_p_kernel(tc, x_words, x_scales, hT, offs, out):
 
         ex = [keep.tile([P, S], F32, name="ex%d" % i) for i in range(TILES)]
         junk = [keep.tile([P, S], F32, name="junk%d" % i, tag="junk%d" % i) for i in range(TILES)]
+        pr = [keep.tile([P, S], F32, name="pr%d" % i) for i in range(TILES)]
         dev = [keep.tile([P, S], F32, name="dev%d" % i) for i in range(TILES)]
         soft = [keep.tile([P, S], F32, name="soft%d" % i) for i in range(TILES)]
         res = [keep.tile([P, S], F32, name="res%d" % i) for i in range(TILES)]
@@ -93,7 +94,7 @@ def tile_picked_ytyp_loc_p_kernel(tc, x_words, x_scales, hT, offs, out):
         total = [column("total", i) for i in range(TILES)]
         inv = [column("inv", i) for i in range(TILES)]
         inv_k = [column("inv_k", i) for i in range(TILES)]
-        centre = [column("centre", i) for i in range(TILES)]
+        centre, spread = {}, {}
         level = [column("level", i) for i in range(TILES)]
 
         acc = [psum.tile([P, S], F32, name="acc%d" % i) for i in range(TILES)]
@@ -130,22 +131,31 @@ def tile_picked_ytyp_loc_p_kernel(tc, x_words, x_scales, hT, offs, out):
             nc.scalar.activation(ex[i][:], neg_y[i][:], ACT.Exp, bias=neg_max[i][:], scale=-1.0, accum_out=total[i][:])
 
         def centre_of(i):
+            centre[i] = keep.tile([P, 1], F32, name="centre%d" % i, tag="sums0" if i == 2 else "centre%d" % i)
             nc.vector.reciprocal(inv[i][:], total[i][:])
-            nc.vector.tensor_scalar(inv_k[i][:], inv[i][:], (1.0 if i == 0 else -1.5) * BIAS_PER_SUM, None, ALU.mult)
             nc.vector.scalar_tensor_tensor(
-                junk[i][:], neg_y[i][:] if i == 0 else acc[i][:], inv_k[i][:], ex[i][:], ALU.mult, ALU.mult, accum_out=centre[i][:]
+                junk[i][:],
+                neg_y[i][:] if i == 0 else acc[i][:],
+                -1.0 if i == 0 else 1.5,
+                ex[i][:],
+                ALU.mult,
+                ALU.mult,
+                accum_out=centre[i][:],
             )
 
         def distance(i):
-            nc.scalar.activation(
-                dev[i][:], neg_y[i][:], ACT.Abs, bias=centre[i][:], scale=-BIAS_PER_SUM, accum_out=level[i][:]
-            )
+            spread[i] = keep.tile([P, 1], F32, name="spread%d" % i, tag="sums0" if i == 0 else "spread%d" % i)
+            nc.scalar.activation(dev[i][:], neg_y[i][:], ACT.Abs, bias=centre[i][:], scale=total[i][:], accum_out=spread[i][:])
 
         def percent(i):
-            nc.vector.tensor_scalar(pr[i], ex[i][:], inv[i][:], 50.0, ALU.mult, ALU.mult)
+            nc.gpsimd.tensor_scalar(pr[i][:], ex[i][:], inv[i][:], 50.0, ALU.mult, ALU.mult)
+
+        def threshold(i):
+            nc.vector.tensor_scalar(inv_k[i][:], inv[i][:], -2.0, None, ALU.mult)
+            nc.vector.tensor_scalar(level[i][:], spread[i][:], inv[i][:], BIAS_PER_SUM, ALU.mult, ALU.mult)
 
         def choice(i, cols):
-            nc.scalar.activation(soft[i][:, cols], dev[i][:, cols], ACT.Tanh, bias=level[i][:], scale=-2.0 / BIAS_PER_SUM)
+            nc.scalar.activation(soft[i][:, cols], dev[i][:, cols], ACT.Tanh, bias=level[i][:], scale=inv_k[i][:])
 
         def finish(i, cols):
             nc.vector.scalar_tensor_tensor(res[i][:, cols], soft[i][:, cols], 1.0, pr[i][:, cols], ALU.add, ALU.mult)
@@ -160,16 +170,14 @@ def tile_picked_ytyp_loc_p_kernel(tc, x_words, x_scales, hT, offs, out):
                 logits(i + 2)
                 exponent(i + 2)
             centre_of(i)
-            if i >= 2:
-                choice(i - 2, whole)
-            distance(i)
-        pr_all = keep.tile([P, TILES * S], F32, name="pr_all", tag="junk2")
-        pr = [pr_all[:, i * S : (i + 1) * S] for i in range(TILES)]
-        for i in range(TILES - 2):
             percent(i)
+            distance(i)
+            threshold(i)
+            if 1 <= i < TILES - 1:
+                choice(i - 1, whole)
+        for i in range(TILES - 2):
             finish(i, whole)
         for i in range(TILES - 2, TILES):
-            percent(i)
             for cols in halves:
                 choice(i, cols)
                 finish(i, cols)

@@ -17,9 +17,14 @@ ACT = mybir.ActivationFunctionType
 
 P = 128
 PACK = 4
+QUADRANT = 32
+LIST_ROWS = 16
+LINE = 4
 TILES = V // P
 HALF = S // 2
-BIAS_PER_SUM = 0.5 * 4.0 * 0.8 / S
+LOGIT_SCALE = 1.5
+DEV_SCALE = 0.5 * 4.0 * 0.8 / S
+LEAD = 2
 
 
 def tile_picked_ytyp_loc_p_kernel(tc, x_words, x_scales, hT, offs, out):
@@ -28,25 +33,26 @@ def tile_picked_ytyp_loc_p_kernel(tc, x_words, x_scales, hT, offs, out):
         keep = ctx.enter_context(tc.tile_pool(name="keep", bufs=1))
         psum = ctx.enter_context(tc.psum_pool(name="psum", bufs=1))
 
-        offsets = keep.tile([P, S // 16], U16, name="offsets")
-        words = keep.tile([P, T], I32, name="words", tag="after_words", align_bytes=64)
-        plane = keep.tile([P, T], U8, name="plane", tag="after_plane", align_bytes=64)
+        offsets = keep.tile([P, S // LIST_ROWS], U16, name="offsets")
+        words = keep.tile([P, T], I32, name="words", align_bytes=64)
+        plane = keep.tile([P, T], U8, name="plane", tag="plane", align_bytes=64)
         warm = keep.tile([P, 2], F32, name="warm")
 
         nc.vector.memset(plane[:].bitcast(I32), 0)
         nc.vector.memset(warm[:, 0:1], 0.0)
         nc.sync.dma_start(offsets[:], offs)
         nc.scalar.activation(warm[:, 1:2], warm[:, 0:1], ACT.Exp)
+
         h_rows = hT.rearrange("(p j) w -> p j w", j=PACK)
-        raw0 = keep.tile([P, PACK, P], F32, name="raw0")
-        raw1 = keep.tile([P, PACK, 2 * P], F32, name="raw1")
-        raw2 = keep.tile([P, PACK, P], F32, name="raw2")
-        nc.sync.dma_start(raw0[:], h_rows[:, :, 0:P])
-        for q in range(4):
-            nc.sync.dma_start(plane[32 * q : 32 * q + 4, :].bitcast(I32), x_scales[0, 4 * q : 4 * q + 4, :].bitcast(I32))
-        nc.sync.dma_start(raw1[:], h_rows[:, :, P : 3 * P])
+        raw = [keep.tile([P, PACK, P], F32, name="raw%d" % i) for i in range(TILES)]
+        nc.sync.dma_start(raw[0][:], h_rows[:, :, 0:P])
+        for q in range(P // QUADRANT):
+            nc.sync.dma_start(
+                plane[QUADRANT * q : QUADRANT * q + 4, :].bitcast(I32), x_scales[0, 4 * q : 4 * q + 4, :].bitcast(I32)
+            )
         nc.sync.dma_start(words[:], x_words[0].rearrange("p n t -> p (n t)").bitcast(I32))
-        nc.sync.dma_start(raw2[:], h_rows[:, :, 3 * P : V])
+        for i in range(1, TILES):
+            nc.sync.dma_start(raw[i][:], h_rows[:, :, i * P : (i + 1) * P])
 
         x_bytes = keep.tile([P, S], U8, name="x_bytes", align_bytes=64)
         x_codes = keep.tile([P, S], U32, name="x_codes", align_bytes=64)
@@ -54,26 +60,23 @@ def tile_picked_ytyp_loc_p_kernel(tc, x_words, x_scales, hT, offs, out):
 
         h_codes, h_bytes = [], []
 
-        def quantise(raw, staged_tag, codes_tag):
-            tiles = 1
-            width = P
-            grouped = keep.tile([P, width * PACK], BF16, name="grouped", tag=staged_tag, align_bytes=64)
+        def quantise(i):
+            grouped = keep.tile([P, P * PACK], BF16, name="grouped", tag="staged%d" % i, align_bytes=64)
             nc.scalar.copy(
-                grouped[:].rearrange("p (c i t) -> p c t i", i=4, t=PACK),
-                raw.rearrange("p t (c i) -> p c t i", i=4),
+                grouped[:].rearrange("p (c n j) -> p c j n", n=LINE, j=PACK),
+                raw[i][:].rearrange("p j (c n) -> p c j n", n=LINE),
             )
-            codes = keep.tile([P, width], U32, name="h_codes", tag=codes_tag, align_bytes=64)
-            scales = keep.tile([P, width], U8, name="h_bytes%d" % len(h_codes), align_bytes=64)
+            codes = keep.tile([P, P], U32, name="h_codes", tag="plane" if i == 0 else "codes%d" % i, align_bytes=64)
+            scales = keep.tile([P, P], U8, name="h_bytes%d" % i, align_bytes=64)
             nc.vector.quantize_mx(out=codes[:].bitcast(FP8X4), scales=scales[:], in_=grouped[:])
-            for j in range(tiles):
-                h_codes.append(codes[:, j * P : (j + 1) * P])
-                h_bytes.append(scales[:, j * P : (j + 1) * P])
+            h_codes.append(codes)
+            h_bytes.append(scales)
 
-        def product(i, acc, cols):
+        def product(i, cols):
             nc.tensor.matmul_mx(
-                out=acc,
-                lhsT=h_codes[i].bitcast(FP8X4),
-                lhsT_scale=h_bytes[i],
+                out=acc[i][:, cols],
+                lhsT=h_codes[i][:].bitcast(FP8X4),
+                lhsT_scale=h_bytes[i][:],
                 rhs=x_codes[:, cols].bitcast(FP8X4),
                 rhs_scale=x_bytes[:, cols],
                 start=True,
@@ -81,103 +84,79 @@ def tile_picked_ytyp_loc_p_kernel(tc, x_words, x_scales, hT, offs, out):
             )
 
         ex = [keep.tile([P, S], F32, name="ex%d" % i) for i in range(TILES)]
-        junk = [keep.tile([P, S], F32, name="junk%d" % i, tag="junk%d" % i) for i in range(TILES)]
-        pr = [keep.tile([P, S], F32, name="pr%d" % i) for i in range(TILES)]
+        terms = [keep.tile([P, S], F32, name="terms%d" % i) for i in range(TILES)]
+        pct = [keep.tile([P, S], F32, name="pct%d" % i) for i in range(TILES)]
         dev = [keep.tile([P, S], F32, name="dev%d" % i) for i in range(TILES)]
         soft = [keep.tile([P, S], F32, name="soft%d" % i) for i in range(TILES)]
         res = [keep.tile([P, S], F32, name="res%d" % i) for i in range(TILES)]
 
-        def column(label, i):
-            return keep.tile([P, 1], F32, name="%s%d" % (label, i))
+        def columns(label):
+            return [keep.tile([P, 1], F32, name="%s%d" % (label, i)) for i in range(TILES)]
 
-        neg_max = [column("neg_max", i) for i in range(TILES)]
-        total = [column("total", i) for i in range(TILES)]
-        inv = [column("inv", i) for i in range(TILES)]
-        inv_k = [column("inv_k", i) for i in range(TILES)]
-        centre, spread = {}, {}
-        level = [column("level", i) for i in range(TILES)]
+        neg_max = columns("neg_max")
+        total = columns("total")
+        inv = columns("inv")
+        weight = columns("weight")
+        centre = columns("centre")
+        level = columns("level")
 
         acc = [psum.tile([P, S], F32, name="acc%d" % i) for i in range(TILES)]
-        late = psum.tile([P, HALF], F32, name="late")
+        whole = slice(0, S)
         halves = [slice(0, HALF), slice(HALF, S)]
-        first = [acc[0][:, halves[0]], late[:]]
-        quantise(raw0[:], "staged0", "after_plane")
-        quantise(raw1[:, :, 0:P], "staged1", "codes1")
-        for u, cols in enumerate(halves):
-            nc.vector.tensor_copy(
-                x_codes[:, cols], words[:].bitcast(U32).indirect(offsets[:, u * HALF // 16 : (u + 1) * HALF // 16])
-            )
-            product(0, first[u], cols)
-        quantise(raw1[:, :, P : 2 * P], "staged2", "after_words")
-        quantise(raw2[:], "staged3", "codes3")
+        quantise(0)
+        for cols in halves:
+            picks = offsets[:, cols.start // LIST_ROWS : cols.stop // LIST_ROWS]
+            nc.vector.tensor_copy(x_codes[:, cols], words[:].bitcast(U32).indirect(picks))
+            product(0, cols)
         for i in range(1, TILES):
-            product(i, acc[i][:], slice(0, S))
+            quantise(i)
+            product(i, whole)
 
         neg_y = [
-            keep.tile([P, S], F32, name="neg_y%d" % i, tag="staged3" if i == 0 else "neg_y%d" % i, align_bytes=64)
-            for i in range(TILES)
+            keep.tile([P, S], F32, name="neg_y%d" % i, tag="staged%d" % (i + 2), align_bytes=64) for i in range(TILES)
         ]
 
-        half_max = column("half_max", 0)
-
         def logits(i):
-            if i == 0:
-                nc.vector.tensor_scalar(neg_y[0][:, halves[0]], first[0], -1.5, None, ALU.mult, ALU.min, accum_out=half_max[:])
-                nc.vector.tensor_scalar(neg_y[0][:, halves[1]], first[1], -1.5, half_max[:], ALU.mult, ALU.min, accum_out=neg_max[0][:])
-                return
-            nc.vector.tensor_scalar(neg_y[i][:], acc[i][:], -1.5, None, ALU.mult, ALU.min, accum_out=neg_max[i][:])
+            nc.vector.tensor_scalar(neg_y[i][:], acc[i][:], -LOGIT_SCALE, None, ALU.mult, ALU.min, accum_out=neg_max[i][:])
 
         def exponent(i):
             nc.scalar.activation(ex[i][:], neg_y[i][:], ACT.Exp, bias=neg_max[i][:], scale=-1.0, accum_out=total[i][:])
 
-        def centre_of(i):
-            centre[i] = keep.tile([P, 1], F32, name="centre%d" % i, tag="sums0" if i == 2 else "centre%d" % i)
+        def weighted_mean(i):
             nc.vector.reciprocal(inv[i][:], total[i][:])
+            nc.vector.tensor_scalar(weight[i][:], inv[i][:], -LOGIT_SCALE * DEV_SCALE, None, ALU.mult)
             nc.vector.scalar_tensor_tensor(
-                junk[i][:],
-                neg_y[i][:] if i == 0 else acc[i][:],
-                -1.0 if i == 0 else 1.5,
-                ex[i][:],
-                ALU.mult,
-                ALU.mult,
-                accum_out=centre[i][:],
+                terms[i][:], acc[i][:], weight[i][:], ex[i][:], ALU.mult, ALU.mult, accum_out=centre[i][:]
             )
 
         def distance(i):
-            spread[i] = keep.tile([P, 1], F32, name="spread%d" % i, tag="sums0" if i == 0 else "spread%d" % i)
-            nc.scalar.activation(dev[i][:], neg_y[i][:], ACT.Abs, bias=centre[i][:], scale=total[i][:], accum_out=spread[i][:])
+            nc.scalar.activation(dev[i][:], neg_y[i][:], ACT.Abs, bias=centre[i][:], scale=-DEV_SCALE, accum_out=level[i][:])
 
         def percent(i):
-            nc.gpsimd.tensor_scalar(pr[i][:], ex[i][:], inv[i][:], 50.0, ALU.mult, ALU.mult)
-
-        def threshold(i):
-            nc.vector.tensor_scalar(inv_k[i][:], inv[i][:], -2.0, None, ALU.mult)
-            nc.vector.tensor_scalar(level[i][:], spread[i][:], inv[i][:], BIAS_PER_SUM, ALU.mult, ALU.mult)
+            nc.gpsimd.tensor_scalar(pct[i][:], ex[i][:], inv[i][:], 50.0, ALU.mult, ALU.mult)
 
         def choice(i, cols):
-            nc.scalar.activation(soft[i][:, cols], dev[i][:, cols], ACT.Tanh, bias=level[i][:], scale=inv_k[i][:])
+            nc.scalar.activation(soft[i][:, cols], dev[i][:, cols], ACT.Tanh, bias=level[i][:], scale=-2.0 / DEV_SCALE)
 
         def finish(i, cols):
-            nc.vector.scalar_tensor_tensor(res[i][:, cols], soft[i][:, cols], 1.0, pr[i][:, cols], ALU.add, ALU.mult)
+            nc.vector.scalar_tensor_tensor(res[i][:, cols], soft[i][:, cols], 1.0, pct[i][:, cols], ALU.add, ALU.mult)
             nc.sync.dma_start(out[i * P : (i + 1) * P, cols], res[i][:, cols])
 
-        whole = slice(0, S)
-        for i in range(2):
+        for i in range(LEAD):
             logits(i)
             exponent(i)
         for i in range(TILES):
-            if i + 2 < TILES:
-                logits(i + 2)
-                exponent(i + 2)
-            centre_of(i)
+            if i + LEAD < TILES:
+                logits(i + LEAD)
+                exponent(i + LEAD)
+            weighted_mean(i)
             percent(i)
+            if i >= LEAD:
+                choice(i - LEAD, whole)
             distance(i)
-            threshold(i)
-            if 1 <= i < TILES - 1:
-                choice(i - 1, whole)
-        for i in range(TILES - 2):
+        for i in range(TILES - LEAD):
             finish(i, whole)
-        for i in range(TILES - 2, TILES):
+        for i in range(TILES - LEAD, TILES):
             for cols in halves:
                 choice(i, cols)
                 finish(i, cols)

from contextlib import ExitStack

import concourse.mybir as mybir

K, T, S, V = 512, 1024, 512, 512
FLOPS = 2 * K * S * V

F32 = mybir.dt.float32
BF16 = mybir.dt.bfloat16
I32 = mybir.dt.int32
U32 = mybir.dt.uint32
U16 = mybir.dt.uint16
U8 = mybir.dt.uint8
FP8X4 = mybir.dt.float8_e4m3fn_x4
ALU = mybir.AluOpType
ACT = mybir.ActivationFunctionType

P = 128
PACK = 4
QUADRANT = 32
LIST_ROWS = 16
LINE = 4
TILES = V // P
HALF = S // 2
LOGIT_SCALE = 1.5
DEV_SCALE = 0.5 * 4.0 * 0.8 / S
LEAD = 2


def tile_picked_ytyp_loc_p_kernel(tc, x_words, x_scales, hT, offs, out):
    nc = tc.nc
    with ExitStack() as ctx:
        keep = ctx.enter_context(tc.tile_pool(name="keep", bufs=1))
        psum = ctx.enter_context(tc.psum_pool(name="psum", bufs=1))

        offsets = keep.tile([P, S // LIST_ROWS], U16, name="offsets")
        words = keep.tile([P, T], I32, name="words", align_bytes=64)
        plane = keep.tile([P, T], U8, name="plane", tag="plane", align_bytes=64)
        warm = keep.tile([P, 2], F32, name="warm")

        nc.vector.memset(plane[:].bitcast(I32), 0)
        nc.vector.memset(warm[:, 0:1], 0.0)
        nc.sync.dma_start(offsets[:], offs)
        nc.scalar.activation(warm[:, 1:2], warm[:, 0:1], ACT.Exp)

        h_rows = hT.rearrange("(p j) w -> p j w", j=PACK)
        raw = [keep.tile([P, PACK, P], F32, name="raw%d" % i) for i in range(TILES)]
        nc.sync.dma_start(raw[0][:], h_rows[:, :, 0:P])
        for q in range(P // QUADRANT):
            nc.sync.dma_start(
                plane[QUADRANT * q : QUADRANT * q + 4, :].bitcast(I32), x_scales[0, 4 * q : 4 * q + 4, :].bitcast(I32)
            )
        nc.sync.dma_start(words[:], x_words[0].rearrange("p n t -> p (n t)").bitcast(I32))
        for i in range(1, TILES):
            nc.sync.dma_start(raw[i][:], h_rows[:, :, i * P : (i + 1) * P])

        x_bytes = keep.tile([P, S], U8, name="x_bytes", align_bytes=64)
        x_codes = keep.tile([P, S], U32, name="x_codes", align_bytes=64)
        nc.vector.tensor_copy(x_bytes[:], plane[:].indirect(offsets[:]))

        h_codes, h_bytes = [], []

        def quantise(i):
            grouped = keep.tile([P, P * PACK], BF16, name="grouped", tag="staged%d" % i, align_bytes=64)
            nc.scalar.copy(
                grouped[:].rearrange("p (c n j) -> p c j n", n=LINE, j=PACK),
                raw[i][:].rearrange("p j (c n) -> p c j n", n=LINE),
            )
            codes = keep.tile([P, P], U32, name="h_codes", tag="plane" if i == 0 else "codes%d" % i, align_bytes=64)
            scales = keep.tile([P, P], U8, name="h_bytes%d" % i, align_bytes=64)
            nc.vector.quantize_mx(out=codes[:].bitcast(FP8X4), scales=scales[:], in_=grouped[:])
            h_codes.append(codes)
            h_bytes.append(scales)

        def product(i, cols):
            nc.tensor.matmul_mx(
                out=acc[i][:, cols],
                lhsT=h_codes[i][:].bitcast(FP8X4),
                lhsT_scale=h_bytes[i][:],
                rhs=x_codes[:, cols].bitcast(FP8X4),
                rhs_scale=x_bytes[:, cols],
                start=True,
                stop=True,
            )

        ex = [keep.tile([P, S], F32, name="ex%d" % i) for i in range(TILES)]
        terms = [keep.tile([P, S], F32, name="terms%d" % i) for i in range(TILES)]
        pct = [keep.tile([P, S], F32, name="pct%d" % i) for i in range(TILES)]
        dev = [keep.tile([P, S], F32, name="dev%d" % i) for i in range(TILES)]
        soft = [keep.tile([P, S], F32, name="soft%d" % i) for i in range(TILES)]
        res = [keep.tile([P, S], F32, name="res%d" % i) for i in range(TILES)]

        def columns(label):
            return [keep.tile([P, 1], F32, name="%s%d" % (label, i)) for i in range(TILES)]

        neg_max = columns("neg_max")
        total = columns("total")
        inv = columns("inv")
        weight = columns("weight")
        centre = columns("centre")
        level = columns("level")

        acc = [psum.tile([P, S], F32, name="acc%d" % i) for i in range(TILES)]
        whole = slice(0, S)
        halves = [slice(0, HALF), slice(HALF, S)]
        quantise(0)
        for cols in halves:
            picks = offsets[:, cols.start // LIST_ROWS : cols.stop // LIST_ROWS]
            nc.vector.tensor_copy(x_codes[:, cols], words[:].bitcast(U32).indirect(picks))
            product(0, cols)
        for i in range(1, TILES):
            quantise(i)
            product(i, whole)

        neg_y = [
            keep.tile([P, S], F32, name="neg_y%d" % i, tag="staged%d" % (i + 2), align_bytes=64) for i in range(TILES)
        ]

        def logits(i):
            nc.vector.tensor_scalar(neg_y[i][:], acc[i][:], -LOGIT_SCALE, None, ALU.mult, ALU.min, accum_out=neg_max[i][:])

        def exponent(i):
            nc.scalar.activation(ex[i][:], neg_y[i][:], ACT.Exp, bias=neg_max[i][:], scale=-1.0, accum_out=total[i][:])

        def weighted_mean(i):
            nc.vector.reciprocal(inv[i][:], total[i][:])
            nc.vector.tensor_scalar(weight[i][:], inv[i][:], -LOGIT_SCALE * DEV_SCALE, None, ALU.mult)
            nc.vector.scalar_tensor_tensor(
                terms[i][:], acc[i][:], weight[i][:], ex[i][:], ALU.mult, ALU.mult, accum_out=centre[i][:]
            )

        def distance(i):
            nc.scalar.activation(dev[i][:], neg_y[i][:], ACT.Abs, bias=centre[i][:], scale=-DEV_SCALE, accum_out=level[i][:])

        def percent(i):
            nc.gpsimd.tensor_scalar(pct[i][:], ex[i][:], inv[i][:], 50.0, ALU.mult, ALU.mult)

        def choice(i, cols):
            nc.scalar.activation(soft[i][:, cols], dev[i][:, cols], ACT.Tanh, bias=level[i][:], scale=-2.0 / DEV_SCALE)

        def finish(i, cols):
            nc.vector.scalar_tensor_tensor(res[i][:, cols], soft[i][:, cols], 1.0, pct[i][:, cols], ALU.add, ALU.mult)
            nc.sync.dma_start(out[i * P : (i + 1) * P, cols], res[i][:, cols])

        for i in range(LEAD):
            logits(i)
            exponent(i)
        for i in range(TILES):
            if i + LEAD < TILES:
                logits(i + LEAD)
                exponent(i + LEAD)
            weighted_mean(i)
            percent(i)
            if i >= LEAD:
                choice(i - LEAD, whole)
            distance(i)
        for i in range(TILES - LEAD):
            finish(i, whole)
        for i in range(TILES - LEAD, TILES):
            for cols in halves:
                choice(i, cols)
                finish(i, cols)
